import numpy as np
import ml_dtypes


def mxq(x, axis, fmt="e4m3"):
    dtype, down = {"e4m3": (ml_dtypes.float8_e4m3fn, 7), "e5m2": (ml_dtypes.float8_e5m2, 14)}[fmt]
    v = np.moveaxis(np.asarray(x, np.float32).astype(ml_dtypes.bfloat16).astype(np.float64), axis, -1)
    blocks = v.reshape(v.shape[:-1] + (-1, 32))
    amax = np.abs(blocks).max(-1, keepdims=True)
    byte = np.maximum(np.where(amax > 0, np.frexp(amax)[1] - 1 + 127, 0) - down, 1)
    scale = np.exp2(byte - 127.0)
    codes = (blocks / scale).astype(np.float32).astype(dtype).astype(np.float64)
    return np.moveaxis((codes * scale).reshape(v.shape), -1, axis)


WIDE = False


def mx_kscale(k):
    if not WIDE:
        return np.ones(k)
    levels = np.array([10, -10, 5, -5, 0])
    if k % 512:
        return np.exp2(np.random.permutation(np.resize(levels, k // 32))).repeat(32)
    a = np.empty((k // 512, 16))
    for p in range(k // 512):
        a[p, :8] = np.random.permutation(np.resize(levels, 8))
        for g in range(8):
            far = levels[np.abs(levels - a[p, g]) >= 10]
            a[p, g + 8] = far[np.random.randint(len(far))]
    return np.exp2(a.ravel()).repeat(32)


def f64(x):
    return np.asarray(x).astype(np.float64)


def striped(idx):
    return np.tile(idx.reshape(-1, 16).T, (8, 1)).astype(np.uint16)


def unstriped(offs):
    return offs[:16].T.reshape(-1).astype(np.int64)


E2M1 = np.array([0.0, 0.5, 1.0, 1.5, 2.0, 3.0, 4.0, 6.0, -0.0, -0.5, -1.0, -1.5, -2.0, -3.0, -4.0, -6.0])


def pack_weight(w, fmt):
    k, n = w.shape
    w = f64(np.asarray(w, np.float32).astype(ml_dtypes.bfloat16)).reshape(k // 32, 32, n)
    amax = np.abs(w).max(1)
    if fmt == "e4m3":
        byte = np.frexp(amax)[1] - 1 + 127 - 7
    else:
        mant, ex = np.frexp(amax / 6.0)
        byte = np.where(mant > 0.5, ex, ex - 1) + 127
    byte = np.clip(np.where(amax > 0, byte, 1), 1, 254)
    scaled = (w * np.exp2(127.0 - byte)[:, None, :]).reshape(k, n).astype(np.float32)
    by_word = np.ascontiguousarray(scaled.reshape(k // 512, 128, 4, n).transpose(0, 1, 3, 2))
    if fmt == "e4m3":
        words = by_word.astype(ml_dtypes.float8_e4m3fn).view(np.uint8)
    else:
        c = by_word.astype(ml_dtypes.float4_e2m1fn).view(np.uint8) & 0xF
        words = (c[..., 0::2] | (c[..., 1::2] << 4)).reshape(k // 512, 128, 2 * n)
    return np.ascontiguousarray(words), np.ascontiguousarray(byte.astype(np.uint8).reshape(k // 512, 16, n))


def unpack_weight(words, scales, fmt):
    g, _, n = scales.shape
    words = np.ascontiguousarray(words).reshape(g, 128, n, -1)
    if fmt == "e4m3":
        vals = words.view(ml_dtypes.float8_e4m3fn).astype(np.float64)
    else:
        nib = np.empty((g, 128, n, 4), np.uint8)
        nib[..., 0::2] = words & 0xF
        nib[..., 1::2] = words >> 4
        vals = E2M1[nib]
    vals = vals * np.repeat(np.exp2(scales.astype(np.float64) - 127.0), 8, axis=1)[..., None]
    return vals.transpose(0, 1, 3, 2).reshape(g * 512, n)


def gelu(v):
    return 0.5 * v * (1.0 + np.tanh(np.sqrt(2.0 / np.pi) * (v + 0.044715 * v**3)))


K, T, E, C, H, N = 512, 1024, 6, 256, 512, 256


def by_expert(wq, xq):
    return np.concatenate([wq[e].T @ xq[:, e * C:(e + 1) * C] for e in range(E)], axis=1)


def setup_inputs():
    n = np.random.standard_normal
    s = mx_kscale(K)
    u = mx_kscale(H)
    slot_token = np.concatenate([np.random.permutation(T)[:C] for e in range(E)])
    partner = np.concatenate([np.random.permutation(T) for _ in range(-(-E * C // T))])[:E * C]
    x = pack_weight(n((K, T)) * s[:, None], "e4m3")
    w1 = [pack_weight(m, "e2m1") for m in n((E, K, H)) / np.sqrt(K) / s[None, :, None] * u]
    wp = [pack_weight(m, "e4m3") for m in n((E, K, H)) / np.sqrt(K) / s[None, :, None] * u]
    w2 = [pack_weight(m, "e2m1") for m in n((E, H, N)) / np.sqrt(H) / u[None, :, None]]
    return {
        "x_words": x[0],
        "x_scales": x[1],
        "w1_words": np.stack([m[0] for m in w1]),
        "w1_scales": np.stack([m[1] for m in w1]),
        "wp_words": np.stack([m[0] for m in wp]),
        "wp_scales": np.stack([m[1] for m in wp]),
        "w2_words": np.stack([m[0] for m in w2]),
        "w2_scales": np.stack([m[1] for m in w2]),
        "offs": striped(slot_token),
        "offs2": striped(partner),
    }


def reference(x_words, x_scales, w1_words, w1_scales, wp_words, wp_scales, w2_words, w2_scales, offs, offs2):
    w1 = np.stack([unpack_weight(w1_words[e], w1_scales[e], "e2m1") for e in range(E)])
    wp = np.stack([unpack_weight(wp_words[e], wp_scales[e], "e4m3") for e in range(E)])
    w2 = np.stack([unpack_weight(w2_words[e], w2_scales[e], "e2m1") for e in range(E)])
    idx, idx2 = unstriped(offs), unstriped(offs2)
    x = unpack_weight(x_words, x_scales, "e4m3")
    h = gelu(by_expert(w1, x[:, idx]) + by_expert(wp, x[:, idx2]))
    y = by_expert(w2, mxq(h, 0, "e4m3"))
    out = y
    return out

@@ -1,0 +1,228 @@
+from contextlib import ExitStack
+
+import concourse.mybir as mybir
+from concourse.masks import make_identity
+
+K, T, E, C, H, N = 512, 1024, 6, 256, 512, 256
+FLOPS = 2 * E * C * (2 * K * H + H * N)
+
+F32 = mybir.dt.float32
+BF16 = mybir.dt.bfloat16
+I32 = mybir.dt.int32
+U32 = mybir.dt.uint32
+U16 = mybir.dt.uint16
+U8 = mybir.dt.uint8
+FP8X4 = mybir.dt.float8_e4m3fn_x4
+FP4X4 = mybir.dt.float4_e2m1fn_x4
+GELU = mybir.ActivationFunctionType.Gelu_apprx_tanh
+
+P = 128
+PER_COL = 16
+WP_ROW = 4
+
+
+def tile_moe_duo_s_gelu_kernel(
+    tc, x_words, x_scales, w1_words, w1_scales, wp_words, wp_scales, w2_words, w2_scales, offs, offs2, out
+):
+    nc = tc.nc
+    with ExitStack() as ctx:
+        held = ctx.enter_context(tc.tile_pool(name="held", bufs=1))
+        ring = ctx.enter_context(tc.tile_pool(name="ring", bufs=1))
+        psum = ctx.enter_context(tc.psum_pool(name="psum", bufs=1))
+
+        tok_list = held.tile([P, E * C // PER_COL], U16, name="tok_list")
+        par_list = held.tile([P, E * C // PER_COL], U16, name="par_list")
+        x_w = held.tile([P, T], I32, name="x_w", align_bytes=64)
+        x_s = held.tile([P, T], U8, name="x_s", align_bytes=64)
+        l1_s = held.tile([P, E, H], U8, name="l1_s", align_bytes=64)
+        w2_s = held.tile([P, E, N], U8, name="w2_s", align_bytes=64)
+        ident = held.tile([P, P], F32, name="ident")
+
+        nc.vector.memset(l1_s[:].rearrange("p e h -> p (e h)").bitcast(I32), 0)
+        make_identity(nc, ident[:])
+        nc.gpsimd.memset(w2_s[:].rearrange("p e h -> p (e h)").bitcast(I32), 0)
+
+        def load_scale_rows(plane, first_row, rows, which=(0, 1, 2, 3), on_sync=4):
+            for r in which:
+                (nc.sync if r < on_sync else nc.gpsimd).dma_start(
+                    plane[first_row + r : P : 32, :, :].bitcast(I32),
+                    rows[:, 0, r:16:4, :].rearrange("e q c -> q e c").bitcast(I32),
+                )
+
+        w1_w, wp_w = {}, {}
+
+        def load_w1(first, last, tag):
+            t = held.tile([P, last - first, 2 * H], U8, name="w1_w%d" % first, tag=tag, align_bytes=64)
+            nc.sync.dma_start(t[:].bitcast(I32), w1_words[first:last, 0].rearrange("e p c -> p e c").bitcast(I32))
+            for e in range(first, last):
+                w1_w[e] = t[:, e - first, :]
+
+        def load_wp(first, last, tag):
+            t = held.tile([P, last - first, H], I32, name="wp_w%d" % first, tag=tag, align_bytes=64)
+            nc.sync.dma_start(t[:], wp_words[first:last, 0].rearrange("e p c d -> p e (c d)").bitcast(I32))
+            for e in range(first, last):
+                wp_w[e] = t[:, e - first, :]
+
+        for q in range(4):
+            rows = x_scales[0, 4 * q : 4 * q + 4, :].rearrange("r t -> (r t)").bitcast(I32)
+            nc.sync.dma_start(x_s[32 * q : 32 * (q + 1), :].bitcast(I32), rows.partition_broadcast(8))
+        nc.sync.dma_start(tok_list[:], offs)
+        nc.sync.dma_start(par_list[:], offs2)
+        load_scale_rows(l1_s, 0, w1_scales, (0,))
+        nc.sync.dma_start(x_w[:], x_words[0].rearrange("p t d -> p (t d)").bitcast(I32))
+        load_wp(0, 1, "wp0")
+        load_w1(0, 2, "w10")
+        load_scale_rows(l1_s, 0, w1_scales, (1, 2, 3))
+        load_scale_rows(l1_s, WP_ROW, wp_scales, (0, 1, 2, 3), 4)
+        load_wp(1, 2, "wp1")
+        w2_w = held.tile([P, E, 2 * N], U8, name="w2_w", align_bytes=64)
+        nc.sync.dma_start(w2_w[:].bitcast(I32), w2_words[:, 0].rearrange("e p c -> p e c").bitcast(I32))
+        load_scale_rows(w2_s, 0, w2_scales)
+        load_wp(2, 4, "wp2")
+        load_w1(2, 6, "w12")
+        load_wp(4, 6, "wp4")
+
+        out_v = out.rearrange("(a n) j -> n a j", n=P)
+        g = {}
+        REGION = 2560
+        PLACE = {"tw": 0, "ts": 1024, "ps": 1280, "pw": 1536}
+
+        def gather(kind, first_block, blocks, offset=None):
+            lst = tok_list if kind[0] == "t" else par_list
+            words = kind[1] == "w"
+            name = "g%s%d" % (kind, first_block)
+            dt = U32 if words else U8
+            if offset is None:
+                t = held.tile([P, blocks * P], dt, name=name, align_bytes=64)
+            else:
+                t = ring.tile([P, blocks * P], dt, name=name, align_bytes=64, offset=offset)
+            lo = first_block * P // PER_COL
+            offsets = lst[:, lo : lo + blocks * P // PER_COL]
+            window = x_w[:].bitcast(U32) if words else x_s[:]
+            nc.vector.tensor_copy(t[:], window.indirect(offsets))
+            for b in range(blocks):
+                g[kind, first_block + b] = t[:, b * P : (b + 1) * P]
+
+        hid, turned, grouped, codes, cscales, ys = {}, {}, {}, {}, {}, {}
+
+        def first_layer(blk):
+            e = blk // 2
+            hid[blk] = held.tile([P, H], BF16, name="hid%d" % blk, align_bytes=64)
+            acc = psum.tile([P, H], F32, name="acc%d" % blk, tag="acc%d" % (blk % 2))
+            nc.tensor.matmul_mx(
+                out=acc[:], lhsT=g["tw", blk].bitcast(FP8X4), lhsT_scale=g["ts", blk],
+                rhs=w1_w[e].bitcast(FP4X4), rhs_scale=l1_s[:, e, :], start=True, stop=False,
+            )
+            nc.tensor.matmul_mx(
+                out=acc[:], lhsT=g["pw", blk].bitcast(FP8X4), lhsT_scale=g["ps", blk],
+                rhs=wp_w[e].bitcast(FP8X4), rhs_scale=l1_s[WP_ROW:P, e, :], start=False, stop=True,
+            )
+            nc.scalar.activation(
+                hid[blk][:].rearrange("s (u p d) -> s u p d", u=2, d=2),
+                acc[:].rearrange("s (p u d) -> s u p d", u=2, d=2),
+                GELU,
+            )
+
+        def turn(un, b):
+            i, e, b0, nb = un
+            if b == 0:
+                turned[i] = psum.tile([P, nb, 2, P], F32, name="turned%d" % i, tag="turned%d" % (i % 2))
+            pairs = hid[2 * e + b0 + b][:].bitcast(F32)
+            for u in range(2):
+                nc.tensor.transpose(turned[i][:, b, u, :], pairs[:, u * P : (u + 1) * P], ident[:])
+
+        def group(un, on_vector=False):
+            i, e, b0, nb = un
+            grouped[i] = ring.tile([P, 4 * nb * P], BF16, name="grouped%d" % i, align_bytes=64, offset=i * REGION + 256)
+            dst = grouped[i][:].bitcast(F32).rearrange("p (b s u) -> p b s u", b=nb, u=2)
+            src = turned[i][:].rearrange("p b u s -> p b s u")
+            if on_vector:
+                nc.vector.tensor_copy(dst, src)
+            else:
+                nc.scalar.copy(dst, src)
+
+        def quantise(un):
+            i, e, b0, nb = un
+            codes[i] = held.tile([P, nb * P], U32, name="codes%d" % i, align_bytes=64)
+            cscales[i] = held.tile([P, nb * P], U8, name="cscales%d" % i, align_bytes=64)
+            nc.vector.quantize_mx(out=codes[i][:].bitcast(FP8X4), scales=cscales[i][:], in_=grouped[i][:])
+
+        def second_layer(un):
+            i, e, b0, nb = un
+            ys[i] = psum.tile([P, 2, nb * P], F32, name="y%d" % i, tag="y%d" % (i % 3))
+            for a in range(2):
+                nc.tensor.matmul_mx(
+                    out=ys[i][:, a, :], lhsT=w2_w[:, e, 2 * a * P : 2 * (a + 1) * P].bitcast(FP4X4),
+                    lhsT_scale=w2_s[:, e, a * P : (a + 1) * P],
+                    rhs=codes[i][:].bitcast(FP8X4), rhs_scale=cscales[i][:], start=True, stop=True,
+                )
+
+        def store(un, on_vector=False):
+            i, e, b0, nb = un
+            res = held.tile([P, 2, nb * P], F32, name="res%d" % i)
+            if on_vector:
+                nc.vector.tensor_copy(res[:], ys[i][:])
+            else:
+                nc.scalar.copy(res[:], ys[i][:])
+            lo = e * C + b0 * P
+            nc.sync.dma_start(out_v[:, :, lo : lo + nb * P], res[:])
+
+        units = [(e, e, 0, 2) for e in range(E - 1)]
+        last_a, last_b = (E - 1, E - 1, 0, 1), (E, E - 1, 1, 1)
+
+        FIRST = (E + 1) * REGION
+        LAST = 2 * E - 1
+        units += [last_a, last_b]
+
+        def unit_of(blk):
+            return (units[blk // 2], blk % 2) if blk < LAST - 1 else (units[blk - (E - 1)], 0)
+
+        def words_for(j):
+            kind = "pw" if j % 2 == 1 else "tw"
+            blocks = 2 if j < LAST else 1
+            region = (j - 5) // 2
+            gather(kind, j, blocks, region * REGION + PLACE[kind] if j >= 5 else None)
+
+        def scales_after(j):
+            kind = "ts" if j % 2 == 0 else "ps"
+            first = j + 2 - j % 2
+            if first > LAST or first < 4:
+                return
+            region = (j - 5) // 2
+            place = region * REGION + PLACE[kind] if j >= 5 else FIRST + 512 * (j % 2) if j < 4 else FIRST + 1024
+            gather(kind, first, 2, place)
+
+        gather("ts", 0, 4)
+        gather("ps", 0, 4)
+        gather("tw", 0, 1, FIRST)
+        gather("pw", 0, 1, FIRST + 512)
+        gather("tw", 1, 1, FIRST + 1024)
+        for j in range(LAST + 1):
+            e = (j - 5) // 2
+            if j >= 5 and j % 2 == 1:
+                quantise(units[e])
+            if j >= 1:
+                words_for(j)
+                scales_after(j)
+            if j >= 2:
+                turn(*unit_of(j - 2))
+            if j >= 5 and j % 2 == 1:
+                second_layer(units[e])
+            first_layer(j)
+            if j >= 3 and j % 2 == 1:
+                group(units[(j - 3) // 2])
+            if j >= 5 and j % 2 == 1:
+                store(units[e])
+        quantise(units[E - 2])
+        turn(last_a, 0)
+        second_layer(units[E - 2])
+        group(last_a, True)
+        quantise(last_a)
+        turn(last_b, 0)
+        store(units[E - 2])
+        second_layer(last_a)
+        group(last_b, True)
+        quantise(last_b)
+        store(last_a)
+        second_layer(last_b)
+        store(last_b, True)

@@ -35,10 +35,12 @@ def tile_moe_duo_s_gelu_kernel(
         x_w = held.tile([P, T], I32, name="x_w", align_bytes=64)
         x_s = held.tile([P, T], U8, name="x_s", align_bytes=64)
         l1_s = held.tile([P, E, H], U8, name="l1_s", align_bytes=64)
+        wp_s = held.tile([P, E, H], U8, name="wp_s", align_bytes=64)
         w2_s = held.tile([P, E, N], U8, name="w2_s", align_bytes=64)
         ident = held.tile([P, P], F32, name="ident")
 
         nc.vector.memset(l1_s[:].rearrange("p e h -> p (e h)").bitcast(I32), 0)
+        nc.gpsimd.memset(wp_s[:].rearrange("p e h -> p (e h)").bitcast(I32), 0)
         make_identity(nc, ident[:])
         nc.gpsimd.memset(w2_s[:].rearrange("p e h -> p (e h)").bitcast(I32), 0)
 
@@ -70,16 +72,16 @@ def tile_moe_duo_s_gelu_kernel(
         nc.sync.dma_start(par_list[:], offs2)
         load_scale_rows(l1_s, 0, w1_scales, (0,))
         nc.sync.dma_start(x_w[:], x_words[0].rearrange("p t d -> p (t d)").bitcast(I32))
-        load_wp(0, 1, "wp0")
-        load_w1(0, 2, "w10")
         load_scale_rows(l1_s, 0, w1_scales, (1, 2, 3))
-        load_scale_rows(l1_s, WP_ROW, wp_scales, (0, 1, 2, 3), 4)
+        load_w1(0, 2, "w10")
+        load_wp(0, 1, "wp0")
+        load_scale_rows(wp_s, WP_ROW, wp_scales)
         load_wp(1, 2, "wp1")
+        load_w1(2, 6, "w12")
+        load_wp(2, 4, "wp2")
         w2_w = held.tile([P, E, 2 * N], U8, name="w2_w", align_bytes=64)
         nc.sync.dma_start(w2_w[:].bitcast(I32), w2_words[:, 0].rearrange("e p c -> p e c").bitcast(I32))
         load_scale_rows(w2_s, 0, w2_scales)
-        load_wp(2, 4, "wp2")
-        load_w1(2, 6, "w12")
         load_wp(4, 6, "wp4")
 
         out_v = out.rearrange("(a n) j -> n a j", n=P)
@@ -115,7 +117,7 @@ def tile_moe_duo_s_gelu_kernel(
             )
             nc.tensor.matmul_mx(
                 out=acc[:], lhsT=g["pw", blk].bitcast(FP8X4), lhsT_scale=g["ps", blk],
-                rhs=wp_w[e].bitcast(FP8X4), rhs_scale=l1_s[WP_ROW:P, e, :], start=False, stop=True,
+                rhs=wp_w[e].bitcast(FP8X4), rhs_scale=wp_s[WP_ROW:P, e, :], start=False, stop=True,
             )
             nc.scalar.activation(
                 hid[blk][:].rearrange("s (u p d) -> s u p d", u=2, d=2),
@@ -133,7 +135,7 @@ def tile_moe_duo_s_gelu_kernel(
 
         def group(un, on_vector=False):
             i, e, b0, nb = un
-            grouped[i] = ring.tile([P, 4 * nb * P], BF16, name="grouped%d" % i, align_bytes=64, offset=i * REGION + 256)
+            grouped[i] = held.tile([P, 4 * nb * P], BF16, name="grouped%d" % i, align_bytes=64)
             dst = grouped[i][:].bitcast(F32).rearrange("p (b s u) -> p b s u", b=nb, u=2)
             src = turned[i][:].rearrange("p b u s -> p b s u")
             if on_vector:
@@ -144,7 +146,11 @@ def tile_moe_duo_s_gelu_kernel(
         def quantise(un):
             i, e, b0, nb = un
             codes[i] = held.tile([P, nb * P], U32, name="codes%d" % i, align_bytes=64)
-            cscales[i] = held.tile([P, nb * P], U8, name="cscales%d" % i, align_bytes=64)
+            if i < E - 1:
+                j = (4, 6, 8, 9, 10)[i]
+                cscales[i] = ring.tile([P, nb * P], U8, name="cscales%d" % i, align_bytes=64, offset=words_place(j) + 256)
+            else:
+                cscales[i] = held.tile([P, nb * P], U8, name="cscales%d" % i, align_bytes=64)
             nc.vector.quantize_mx(out=codes[i][:].bitcast(FP8X4), scales=cscales[i][:], in_=grouped[i][:])
 
         def second_layer(un):
@@ -170,59 +176,61 @@ def tile_moe_duo_s_gelu_kernel(
         units = [(e, e, 0, 2) for e in range(E - 1)]
         last_a, last_b = (E - 1, E - 1, 0, 1), (E, E - 1, 1, 1)
 
-        FIRST = (E + 1) * REGION
         LAST = 2 * E - 1
+        LANE, STAGGER = 4096, 768
         units += [last_a, last_b]
 
         def unit_of(blk):
-            return (units[blk // 2], blk % 2) if blk < LAST - 1 else (units[blk - (E - 1)], 0)
+            return (units[blk // 2], blk % 2)
+
+        def words_place(j):
+            return j % 3 * LANE + j // 3 * STAGGER
 
         def words_for(j):
-            kind = "pw" if j % 2 == 1 else "tw"
-            blocks = 2 if j < LAST else 1
-            region = (j - 5) // 2
-            gather(kind, j, blocks, region * REGION + PLACE[kind] if j >= 5 else None)
+            gather("pw" if j % 2 else "tw", j, 2 if j < LAST else 1, words_place(j))
 
         def scales_after(j):
-            kind = "ts" if j % 2 == 0 else "ps"
+            kind = "ps" if j % 2 else "ts"
             first = j + 2 - j % 2
             if first > LAST or first < 4:
                 return
-            region = (j - 5) // 2
-            place = region * REGION + PLACE[kind] if j >= 5 else FIRST + 512 * (j % 2) if j < 4 else FIRST + 1024
-            gather(kind, first, 2, place)
+            gather(kind, first, 2, words_place(j) - 256 if j >= 3 else 3 * LANE)
 
         gather("ts", 0, 4)
         gather("ps", 0, 4)
-        gather("tw", 0, 1, FIRST)
-        gather("pw", 0, 1, FIRST + 512)
-        gather("tw", 1, 1, FIRST + 1024)
+        gather("tw", 0, 1, 3 * LANE)
+        gather("pw", 0, 1, 512)
+        gather("tw", 1, 1)
         for j in range(LAST + 1):
-            e = (j - 5) // 2
-            if j >= 5 and j % 2 == 1:
+            e = (j - 7) // 2
+            second = j >= 7 and j % 2 == 1
+            if second:
                 quantise(units[e])
             if j >= 1:
                 words_for(j)
                 scales_after(j)
             if j >= 2:
                 turn(*unit_of(j - 2))
-            if j >= 5 and j % 2 == 1:
-                second_layer(units[e])
-            first_layer(j)
             if j >= 3 and j % 2 == 1:
                 group(units[(j - 3) // 2])
-            if j >= 5 and j % 2 == 1:
-                store(units[e])
-        quantise(units[E - 2])
+            if second:
+                second_layer(units[e])
+            first_layer(j)
+            if second:
+                store(units[e], j == LAST)
+        quantise(units[E - 3])
         turn(last_a, 0)
-        second_layer(units[E - 2])
-        group(last_a, True)
-        quantise(last_a)
+        second_layer(units[E - 3])
+        quantise(units[E - 2])
+        store(units[E - 3], True)
         turn(last_b, 0)
+        group(last_a)
+        second_layer(units[E - 2])
+        quantise(last_a)
+        group(last_b)
+        quantise(last_b)
         store(units[E - 2])
         second_layer(last_a)
-        group(last_b, True)
-        quantise(last_b)
         store(last_a)
         second_layer(last_b)
         store(last_b, True)

@@ -17,8 +17,12 @@ FP4X4 = mybir.dt.float4_e2m1fn_x4
 GELU = mybir.ActivationFunctionType.Gelu_apprx_tanh
 
 P = 128
-PER_COL = 16
+QUADRANT = 32
+PER_COLUMN = 16
 WP_ROW = 4
+BLOCKS = E * C // P
+LANE = 5120
+STAGGER = 768
 
 
 def tile_moe_duo_s_gelu_kernel(
@@ -27,210 +31,187 @@ def tile_moe_duo_s_gelu_kernel(
     nc = tc.nc
     with ExitStack() as ctx:
         held = ctx.enter_context(tc.tile_pool(name="held", bufs=1))
-        ring = ctx.enter_context(tc.tile_pool(name="ring", bufs=1))
+        lanes = ctx.enter_context(tc.tile_pool(name="lanes", bufs=1))
         psum = ctx.enter_context(tc.psum_pool(name="psum", bufs=1))
 
-        tok_list = held.tile([P, E * C // PER_COL], U16, name="tok_list")
-        par_list = held.tile([P, E * C // PER_COL], U16, name="par_list")
+        token_list = held.tile([P, E * C // PER_COLUMN], U16, name="token_list")
+        partner_list = held.tile([P, E * C // PER_COLUMN], U16, name="partner_list")
         x_w = held.tile([P, T], I32, name="x_w", align_bytes=64)
         x_s = held.tile([P, T], U8, name="x_s", align_bytes=64)
-        l1_s = held.tile([P, E, H], U8, name="l1_s", align_bytes=64)
+        w1_s = held.tile([P, E, H], U8, name="w1_s", align_bytes=64)
         wp_s = held.tile([P, E, H], U8, name="wp_s", align_bytes=64)
         w2_s = held.tile([P, E, N], U8, name="w2_s", align_bytes=64)
         ident = held.tile([P, P], F32, name="ident")
 
-        nc.vector.memset(l1_s[:].rearrange("p e h -> p (e h)").bitcast(I32), 0)
-        nc.gpsimd.memset(wp_s[:].rearrange("p e h -> p (e h)").bitcast(I32), 0)
+        nc.vector.memset(w1_s[:].rearrange("p e c -> p (e c)").bitcast(I32), 0)
+        nc.gpsimd.memset(wp_s[:].rearrange("p e c -> p (e c)").bitcast(I32), 0)
         make_identity(nc, ident[:])
-        nc.gpsimd.memset(w2_s[:].rearrange("p e h -> p (e h)").bitcast(I32), 0)
+        nc.gpsimd.memset(w2_s[:].rearrange("p e c -> p (e c)").bitcast(I32), 0)
 
-        def load_scale_rows(plane, first_row, rows, which=(0, 1, 2, 3), on_sync=4):
+        def load_scale_rows(plane, first_row, rows, which):
             for r in which:
-                (nc.sync if r < on_sync else nc.gpsimd).dma_start(
-                    plane[first_row + r : P : 32, :, :].bitcast(I32),
+                nc.sync.dma_start(
+                    plane[first_row + r : P : QUADRANT, :, :].bitcast(I32),
                     rows[:, 0, r:16:4, :].rearrange("e q c -> q e c").bitcast(I32),
                 )
 
-        w1_w, wp_w = {}, {}
-
-        def load_w1(first, last, tag):
-            t = held.tile([P, last - first, 2 * H], U8, name="w1_w%d" % first, tag=tag, align_bytes=64)
-            nc.sync.dma_start(t[:].bitcast(I32), w1_words[first:last, 0].rearrange("e p c -> p e c").bitcast(I32))
+        def load_words(name, words, first, last, into):
+            width = words.shape[2]
+            tile = held.tile([P, last - first, width], U8, name="%s_w%d" % (name, first), align_bytes=64)
+            nc.sync.dma_start(tile[:].bitcast(I32), words[first:last].rearrange("e p c -> p e c").bitcast(I32))
             for e in range(first, last):
-                w1_w[e] = t[:, e - first, :]
+                into[e] = tile[:, e - first, :]
 
-        def load_wp(first, last, tag):
-            t = held.tile([P, last - first, H], I32, name="wp_w%d" % first, tag=tag, align_bytes=64)
-            nc.sync.dma_start(t[:], wp_words[first:last, 0].rearrange("e p c d -> p e (c d)").bitcast(I32))
-            for e in range(first, last):
-                wp_w[e] = t[:, e - first, :]
+        w1_rows = w1_words[:, 0]
+        wp_rows = wp_words[:, 0].rearrange("e p c d -> e p (c d)")
+        w2_rows = w2_words[:, 0]
+        w1_w, wp_w, w2_w = {}, {}, {}
 
+        nc.sync.dma_start(token_list[:], offs)
         for q in range(4):
             rows = x_scales[0, 4 * q : 4 * q + 4, :].rearrange("r t -> (r t)").bitcast(I32)
-            nc.sync.dma_start(x_s[32 * q : 32 * (q + 1), :].bitcast(I32), rows.partition_broadcast(8))
-        nc.sync.dma_start(tok_list[:], offs)
-        nc.sync.dma_start(par_list[:], offs2)
-        load_scale_rows(l1_s, 0, w1_scales, (0,))
+            queue = nc.scalar if q < 2 else nc.sync
+            queue.dma_start(x_s[QUADRANT * q : QUADRANT * (q + 1), :].bitcast(I32), rows.partition_broadcast(8))
+        nc.sync.dma_start(partner_list[:], offs2)
+        load_scale_rows(w1_s, 0, w1_scales, (0,))
         nc.sync.dma_start(x_w[:], x_words[0].rearrange("p t d -> p (t d)").bitcast(I32))
-        load_scale_rows(l1_s, 0, w1_scales, (1, 2, 3))
-        load_w1(0, 2, "w10")
-        load_wp(0, 1, "wp0")
-        load_scale_rows(wp_s, WP_ROW, wp_scales)
-        load_wp(1, 2, "wp1")
-        load_w1(2, 6, "w12")
-        load_wp(2, 4, "wp2")
-        w2_w = held.tile([P, E, 2 * N], U8, name="w2_w", align_bytes=64)
-        nc.sync.dma_start(w2_w[:].bitcast(I32), w2_words[:, 0].rearrange("e p c -> p e c").bitcast(I32))
-        load_scale_rows(w2_s, 0, w2_scales)
-        load_wp(4, 6, "wp4")
+        load_scale_rows(w1_s, 0, w1_scales, (1, 2, 3))
+        load_words("w1", w1_rows, 0, 2, w1_w)
+        load_words("wp", wp_rows, 0, 1, wp_w)
+        load_scale_rows(wp_s, WP_ROW, wp_scales, (0, 1, 2, 3))
+        load_words("wp", wp_rows, 1, 2, wp_w)
+        load_words("w1", w1_rows, 2, E, w1_w)
+        load_words("wp", wp_rows, 2, 4, wp_w)
+        load_words("w2", w2_rows, 0, E, w2_w)
+        load_scale_rows(w2_s, 0, w2_scales, (0, 1, 2, 3))
+        load_words("wp", wp_rows, 4, E, wp_w)
 
-        out_v = out.rearrange("(a n) j -> n a j", n=P)
-        g = {}
-        REGION = 2560
-        PLACE = {"tw": 0, "ts": 1024, "ps": 1280, "pw": 1536}
+        gathered = {}
 
-        def gather(kind, first_block, blocks, offset=None):
-            lst = tok_list if kind[0] == "t" else par_list
-            words = kind[1] == "w"
-            name = "g%s%d" % (kind, first_block)
-            dt = U32 if words else U8
-            if offset is None:
-                t = held.tile([P, blocks * P], dt, name=name, align_bytes=64)
-            else:
-                t = ring.tile([P, blocks * P], dt, name=name, align_bytes=64, offset=offset)
-            lo = first_block * P // PER_COL
-            offsets = lst[:, lo : lo + blocks * P // PER_COL]
-            window = x_w[:].bitcast(U32) if words else x_s[:]
-            nc.vector.tensor_copy(t[:], window.indirect(offsets))
+        def gather(side, sort, first_block, blocks, offset=None):
+            slots = token_list if side == "token" else partner_list
+            window = x_w[:].bitcast(U32) if sort == "words" else x_s[:]
+            pool = held if offset is None else lanes
+            tile = pool.tile(
+                [P, blocks * P], window.dtype, name="%s_%s%d" % (side, sort, first_block), align_bytes=64, offset=offset
+            )
+            columns = slice(first_block * P // PER_COLUMN, (first_block + blocks) * P // PER_COLUMN)
+            nc.vector.tensor_copy(tile[:], window.indirect(slots[:, columns]))
             for b in range(blocks):
-                g[kind, first_block + b] = t[:, b * P : (b + 1) * P]
+                gathered[side, sort, first_block + b] = tile[:, b * P : (b + 1) * P]
 
-        hid, turned, grouped, codes, cscales, ys = {}, {}, {}, {}, {}, {}
+        def lane_offset(last_block):
+            return last_block % 3 * LANE + last_block // 3 * STAGGER + 256
 
-        def first_layer(blk):
-            e = blk // 2
-            hid[blk] = held.tile([P, H], BF16, name="hid%d" % blk, align_bytes=64)
-            acc = psum.tile([P, H], F32, name="acc%d" % blk, tag="acc%d" % (blk % 2))
-            nc.tensor.matmul_mx(
-                out=acc[:], lhsT=g["tw", blk].bitcast(FP8X4), lhsT_scale=g["ts", blk],
-                rhs=w1_w[e].bitcast(FP4X4), rhs_scale=l1_s[:, e, :], start=True, stop=False,
-            )
-            nc.tensor.matmul_mx(
-                out=acc[:], lhsT=g["pw", blk].bitcast(FP8X4), lhsT_scale=g["ps", blk],
-                rhs=wp_w[e].bitcast(FP8X4), rhs_scale=wp_s[WP_ROW:P, e, :], start=False, stop=True,
-            )
+        def gather_words(j):
+            side = "partner" if j % 2 else "token"
+            blocks = min(2, BLOCKS - j)
+            gather(side, "words", j, blocks, lane_offset(j + 1) - 256 * (j < 2))
+
+        def gather_scales(j):
+            first = j + 2 - j % 2
+            if 4 <= first < BLOCKS:
+                gather("partner" if j % 2 else "token", "scales", first, 2, lane_offset(j + 1) - 256)
+
+        hidden, turned, grouped, codes, code_scales, sums = {}, {}, {}, {}, {}, {}
+
+        def first_layer(j):
+            e = j // 2
+            acc = psum.tile([P, H], F32, name="acc%d" % j, tag="acc%d" % (j % 3 if j < 8 else j % 2))
+            passes = [
+                ("token", w1_w[e].bitcast(FP4X4), w1_s[:, e, :]),
+                ("partner", wp_w[e].bitcast(FP8X4), wp_s[WP_ROW:P, e, :]),
+            ]
+            for n, (side, words, scales) in enumerate(passes if j % 2 or j == 0 else passes[::-1]):
+                nc.tensor.matmul_mx(
+                    out=acc[:], lhsT=gathered[side, "words", j].bitcast(FP8X4), lhsT_scale=gathered[side, "scales", j],
+                    rhs=words, rhs_scale=scales, start=(n == 0), stop=(n == 1),
+                )
+            hidden[j] = held.tile([P, H], BF16, name="hidden%d" % j, align_bytes=64)
             nc.scalar.activation(
-                hid[blk][:].rearrange("s (u p d) -> s u p d", u=2, d=2),
+                hidden[j][:].rearrange("s (u p d) -> s u p d", u=2, d=2),
                 acc[:].rearrange("s (p u d) -> s u p d", u=2, d=2),
                 GELU,
             )
 
-        def turn(un, b):
-            i, e, b0, nb = un
+        units = [(2 * e, 2) for e in range(E - 1)] + [(BLOCKS - 2, 1), (BLOCKS - 1, 1)]
+
+        def turn(i, b):
+            first, blocks = units[i]
             if b == 0:
-                turned[i] = psum.tile([P, nb, 2, P], F32, name="turned%d" % i, tag="turned%d" % (i % 2))
-            pairs = hid[2 * e + b0 + b][:].bitcast(F32)
+                turned[i] = psum.tile([P, blocks, 2, P], F32, name="turned%d" % i, tag="bank%d" % (i % 3))
+            pairs = hidden[first + b][:].bitcast(F32)
             for u in range(2):
                 nc.tensor.transpose(turned[i][:, b, u, :], pairs[:, u * P : (u + 1) * P], ident[:])
 
-        def group(un, on_vector=False):
-            i, e, b0, nb = un
-            grouped[i] = held.tile([P, 4 * nb * P], BF16, name="grouped%d" % i, align_bytes=64)
-            dst = grouped[i][:].bitcast(F32).rearrange("p (b s u) -> p b s u", b=nb, u=2)
-            src = turned[i][:].rearrange("p b u s -> p b s u")
-            if on_vector:
-                nc.vector.tensor_copy(dst, src)
-            else:
-                nc.scalar.copy(dst, src)
+        def group(i, copy):
+            blocks = units[i][1]
+            grouped[i] = held.tile([P, 4 * blocks * P], BF16, name="grouped%d" % i, align_bytes=64)
+            copy(
+                grouped[i][:].bitcast(F32).rearrange("p (b s u) -> p b s u", b=blocks, u=2),
+                turned[i][:].rearrange("p b u s -> p b s u"),
+            )
 
-        def quantise(un):
-            i, e, b0, nb = un
-            codes[i] = held.tile([P, nb * P], U32, name="codes%d" % i, align_bytes=64)
-            if i < E - 1:
-                j = (4, 6, 8, 9, 10)[i]
-                cscales[i] = ring.tile([P, nb * P], U8, name="cscales%d" % i, align_bytes=64, offset=words_place(j) + 256)
-            else:
-                cscales[i] = held.tile([P, nb * P], U8, name="cscales%d" % i, align_bytes=64)
-            nc.vector.quantize_mx(out=codes[i][:].bitcast(FP8X4), scales=cscales[i][:], in_=grouped[i][:])
+        def quantise(i, behind_block=None, shift=256):
+            width = units[i][1] * P
+            codes[i] = held.tile([P, width], U32, name="codes%d" % i, align_bytes=64)
+            pool, offset = (held, None) if behind_block is None else (lanes, lane_offset(behind_block) + shift)
+            code_scales[i] = pool.tile([P, width], U8, name="code_scales%d" % i, align_bytes=64, offset=offset)
+            nc.vector.quantize_mx(out=codes[i][:].bitcast(FP8X4), scales=code_scales[i][:], in_=grouped[i][:])
 
-        def second_layer(un):
-            i, e, b0, nb = un
-            ys[i] = psum.tile([P, 2, nb * P], F32, name="y%d" % i, tag="y%d" % (i % 3))
+        def second_layer(i):
+            first, blocks = units[i]
+            e = first // 2
+            sums[i] = psum.tile([P, 2, blocks * P], F32, name="sums%d" % i, tag=("bank2", "bank0", "bank1", "bank3", "bank4", "bank2", "bank0")[i])
             for a in range(2):
                 nc.tensor.matmul_mx(
-                    out=ys[i][:, a, :], lhsT=w2_w[:, e, 2 * a * P : 2 * (a + 1) * P].bitcast(FP4X4),
+                    out=sums[i][:, a, :], lhsT=w2_w[e][:, 2 * a * P : 2 * (a + 1) * P].bitcast(FP4X4),
                     lhsT_scale=w2_s[:, e, a * P : (a + 1) * P],
-                    rhs=codes[i][:].bitcast(FP8X4), rhs_scale=cscales[i][:], start=True, stop=True,
+                    rhs=codes[i][:].bitcast(FP8X4), rhs_scale=code_scales[i][:], start=True, stop=True,
                 )
 
-        def store(un, on_vector=False):
-            i, e, b0, nb = un
-            res = held.tile([P, 2, nb * P], F32, name="res%d" % i)
-            if on_vector:
-                nc.vector.tensor_copy(res[:], ys[i][:])
-            else:
-                nc.scalar.copy(res[:], ys[i][:])
-            lo = e * C + b0 * P
-            nc.sync.dma_start(out_v[:, :, lo : lo + nb * P], res[:])
+        out_rows = out.rearrange("(a n) j -> n a j", n=P)
 
-        units = [(e, e, 0, 2) for e in range(E - 1)]
-        last_a, last_b = (E - 1, E - 1, 0, 1), (E, E - 1, 1, 1)
+        def store(i, copy):
+            first, blocks = units[i]
+            result = held.tile([P, 2, blocks * P], F32, name="result%d" % i)
+            copy(result[:], sums[i][:])
+            nc.sync.dma_start(out_rows[:, :, first * P : (first + blocks) * P], result[:])
 
-        LAST = 2 * E - 1
-        LANE, STAGGER = 4096, 768
-        units += [last_a, last_b]
-
-        def unit_of(blk):
-            return (units[blk // 2], blk % 2)
-
-        def words_place(j):
-            return j % 3 * LANE + j // 3 * STAGGER
-
-        def words_for(j):
-            gather("pw" if j % 2 else "tw", j, 2 if j < LAST else 1, words_place(j))
-
-        def scales_after(j):
-            kind = "ps" if j % 2 else "ts"
-            first = j + 2 - j % 2
-            if first > LAST or first < 4:
-                return
-            gather(kind, first, 2, words_place(j) - 256 if j >= 3 else 3 * LANE)
-
-        gather("ts", 0, 4)
-        gather("ps", 0, 4)
-        gather("tw", 0, 1, 3 * LANE)
-        gather("pw", 0, 1, 512)
-        gather("tw", 1, 1)
-        for j in range(LAST + 1):
-            e = (j - 7) // 2
-            second = j >= 7 and j % 2 == 1
-            if second:
-                quantise(units[e])
+        gather("token", "scales", 0, 4)
+        gather("partner", "scales", 0, 4)
+        gather("token", "words", 0, 2, lane_offset(1) - 256)
+        gather("partner", "words", 0, 1, lane_offset(0) + 256)
+        for j in range(BLOCKS):
+            i = (j - 7) // 2
+            finish = j >= 7 and j % 2 == 1
+            if finish:
+                quantise(i, j - 2)
             if j >= 1:
-                words_for(j)
-                scales_after(j)
+                gather_words(j)
+                gather_scales(j)
             if j >= 2:
-                turn(*unit_of(j - 2))
+                turn((j - 2) // 2, j % 2)
             if j >= 3 and j % 2 == 1:
-                group(units[(j - 3) // 2])
-            if second:
-                second_layer(units[e])
+                group((j - 3) // 2, nc.vector.tensor_copy if j == BLOCKS - 1 else nc.scalar.copy)
+            if finish:
+                second_layer(i)
             first_layer(j)
-            if second:
-                store(units[e], j == LAST)
-        quantise(units[E - 3])
-        turn(last_a, 0)
-        second_layer(units[E - 3])
-        quantise(units[E - 2])
-        store(units[E - 3], True)
-        turn(last_b, 0)
-        group(last_a)
-        second_layer(units[E - 2])
-        quantise(last_a)
-        group(last_b)
-        quantise(last_b)
-        store(units[E - 2])
-        second_layer(last_a)
-        store(last_a)
-        second_layer(last_b)
-        store(last_b, True)
+            if finish:
+                store(i, nc.vector.tensor_copy if j == BLOCKS - 1 else nc.scalar.copy)
+        quantise(3, BLOCKS - 1, 0)
+        turn(5, 0)
+        second_layer(3)
+        quantise(4, BLOCKS - 1)
+        turn(6, 0)
+        group(5, nc.scalar.copy)
+        second_layer(4)
+        quantise(5)
+        group(6, nc.scalar.copy)
+        quantise(6)
+        store(3, nc.scalar.copy)
+        store(4, nc.scalar.copy)
+        second_layer(5)
+        store(5, nc.vector.tensor_copy)
+        second_layer(6)
+        store(6, nc.vector.tensor_copy)

from contextlib import ExitStack

import concourse.mybir as mybir
from concourse.masks import make_identity

K, T, E, C, H, N = 512, 1024, 6, 256, 512, 256
FLOPS = 2 * E * C * (2 * K * H + H * N)

F32 = mybir.dt.float32
BF16 = mybir.dt.bfloat16
I32 = mybir.dt.int32
U32 = mybir.dt.uint32
U16 = mybir.dt.uint16
U8 = mybir.dt.uint8
FP8X4 = mybir.dt.float8_e4m3fn_x4
FP4X4 = mybir.dt.float4_e2m1fn_x4
GELU = mybir.ActivationFunctionType.Gelu_apprx_tanh

P = 128
QUADRANT = 32
PER_COLUMN = 16
WP_ROW = 4
BLOCKS = E * C // P
LANE = 5120
STAGGER = 768


def tile_moe_duo_s_gelu_kernel(
    tc, x_words, x_scales, w1_words, w1_scales, wp_words, wp_scales, w2_words, w2_scales, offs, offs2, out
):
    nc = tc.nc
    with ExitStack() as ctx:
        held = ctx.enter_context(tc.tile_pool(name="held", bufs=1))
        lanes = ctx.enter_context(tc.tile_pool(name="lanes", bufs=1))
        psum = ctx.enter_context(tc.psum_pool(name="psum", bufs=1))

        token_list = held.tile([P, E * C // PER_COLUMN], U16, name="token_list")
        partner_list = held.tile([P, E * C // PER_COLUMN], U16, name="partner_list")
        x_w = held.tile([P, T], I32, name="x_w", align_bytes=64)
        x_s = held.tile([P, T], U8, name="x_s", align_bytes=64)
        w1_s = held.tile([P, E, H], U8, name="w1_s", align_bytes=64)
        wp_s = held.tile([P, E, H], U8, name="wp_s", align_bytes=64)
        w2_s = held.tile([P, E, N], U8, name="w2_s", align_bytes=64)
        ident = held.tile([P, P], F32, name="ident")

        nc.vector.memset(w1_s[:].rearrange("p e c -> p (e c)").bitcast(I32), 0)
        nc.gpsimd.memset(wp_s[:].rearrange("p e c -> p (e c)").bitcast(I32), 0)
        make_identity(nc, ident[:])
        nc.gpsimd.memset(w2_s[:].rearrange("p e c -> p (e c)").bitcast(I32), 0)

        def load_scale_rows(plane, first_row, rows, which):
            for r in which:
                nc.sync.dma_start(
                    plane[first_row + r : P : QUADRANT, :, :].bitcast(I32),
                    rows[:, 0, r:16:4, :].rearrange("e q c -> q e c").bitcast(I32),
                )

        def load_words(name, words, first, last, into):
            width = words.shape[2]
            tile = held.tile([P, last - first, width], U8, name="%s_w%d" % (name, first), align_bytes=64)
            nc.sync.dma_start(tile[:].bitcast(I32), words[first:last].rearrange("e p c -> p e c").bitcast(I32))
            for e in range(first, last):
                into[e] = tile[:, e - first, :]

        w1_rows = w1_words[:, 0]
        wp_rows = wp_words[:, 0].rearrange("e p c d -> e p (c d)")
        w2_rows = w2_words[:, 0]
        w1_w, wp_w, w2_w = {}, {}, {}

        nc.sync.dma_start(token_list[:], offs)
        for q in range(4):
            rows = x_scales[0, 4 * q : 4 * q + 4, :].rearrange("r t -> (r t)").bitcast(I32)
            queue = nc.scalar if q < 2 else nc.sync
            queue.dma_start(x_s[QUADRANT * q : QUADRANT * (q + 1), :].bitcast(I32), rows.partition_broadcast(8))
        nc.sync.dma_start(partner_list[:], offs2)
        load_scale_rows(w1_s, 0, w1_scales, (0,))
        nc.sync.dma_start(x_w[:], x_words[0].rearrange("p t d -> p (t d)").bitcast(I32))
        load_scale_rows(w1_s, 0, w1_scales, (1, 2, 3))
        load_words("w1", w1_rows, 0, 2, w1_w)
        load_words("wp", wp_rows, 0, 1, wp_w)
        load_scale_rows(wp_s, WP_ROW, wp_scales, (0, 1, 2, 3))
        load_words("wp", wp_rows, 1, 2, wp_w)
        load_words("w1", w1_rows, 2, E, w1_w)
        load_words("wp", wp_rows, 2, 4, wp_w)
        load_words("w2", w2_rows, 0, E, w2_w)
        load_scale_rows(w2_s, 0, w2_scales, (0, 1, 2, 3))
        load_words("wp", wp_rows, 4, E, wp_w)

        gathered = {}

        def gather(side, sort, first_block, blocks, offset=None):
            slots = token_list if side == "token" else partner_list
            window = x_w[:].bitcast(U32) if sort == "words" else x_s[:]
            pool = held if offset is None else lanes
            tile = pool.tile(
                [P, blocks * P], window.dtype, name="%s_%s%d" % (side, sort, first_block), align_bytes=64, offset=offset
            )
            columns = slice(first_block * P // PER_COLUMN, (first_block + blocks) * P // PER_COLUMN)
            nc.vector.tensor_copy(tile[:], window.indirect(slots[:, columns]))
            for b in range(blocks):
                gathered[side, sort, first_block + b] = tile[:, b * P : (b + 1) * P]

        def lane_offset(last_block):
            return last_block % 3 * LANE + last_block // 3 * STAGGER + 256

        def gather_words(j):
            side = "partner" if j % 2 else "token"
            blocks = min(2, BLOCKS - j)
            gather(side, "words", j, blocks, lane_offset(j + 1) - 256 * (j < 2))

        def gather_scales(j):
            first = j + 2 - j % 2
            if 4 <= first < BLOCKS:
                gather("partner" if j % 2 else "token", "scales", first, 2, lane_offset(j + 1) - 256)

        hidden, turned, grouped, codes, code_scales, sums = {}, {}, {}, {}, {}, {}

        def first_layer(j):
            e = j // 2
            acc = psum.tile([P, H], F32, name="acc%d" % j, tag="acc%d" % (j % 3 if j < 8 else j % 2))
            passes = [
                ("token", w1_w[e].bitcast(FP4X4), w1_s[:, e, :]),
                ("partner", wp_w[e].bitcast(FP8X4), wp_s[WP_ROW:P, e, :]),
            ]
            for n, (side, words, scales) in enumerate(passes if j % 2 or j == 0 else passes[::-1]):
                nc.tensor.matmul_mx(
                    out=acc[:], lhsT=gathered[side, "words", j].bitcast(FP8X4), lhsT_scale=gathered[side, "scales", j],
                    rhs=words, rhs_scale=scales, start=(n == 0), stop=(n == 1),
                )
            hidden[j] = held.tile([P, H], BF16, name="hidden%d" % j, align_bytes=64)
            nc.scalar.activation(
                hidden[j][:].rearrange("s (u p d) -> s u p d", u=2, d=2),
                acc[:].rearrange("s (p u d) -> s u p d", u=2, d=2),
                GELU,
            )

        units = [(2 * e, 2) for e in range(E - 1)] + [(BLOCKS - 2, 1), (BLOCKS - 1, 1)]

        def turn(i, b):
            first, blocks = units[i]
            if b == 0:
                turned[i] = psum.tile([P, blocks, 2, P], F32, name="turned%d" % i, tag="bank%d" % (i % 3))
            pairs = hidden[first + b][:].bitcast(F32)
            for u in range(2):
                nc.tensor.transpose(turned[i][:, b, u, :], pairs[:, u * P : (u + 1) * P], ident[:])

        def group(i, copy):
            blocks = units[i][1]
            grouped[i] = held.tile([P, 4 * blocks * P], BF16, name="grouped%d" % i, align_bytes=64)
            copy(
                grouped[i][:].bitcast(F32).rearrange("p (b s u) -> p b s u", b=blocks, u=2),
                turned[i][:].rearrange("p b u s -> p b s u"),
            )

        def quantise(i, behind_block=None, shift=256):
            width = units[i][1] * P
            codes[i] = held.tile([P, width], U32, name="codes%d" % i, align_bytes=64)
            pool, offset = (held, None) if behind_block is None else (lanes, lane_offset(behind_block) + shift)
            code_scales[i] = pool.tile([P, width], U8, name="code_scales%d" % i, align_bytes=64, offset=offset)
            nc.vector.quantize_mx(out=codes[i][:].bitcast(FP8X4), scales=code_scales[i][:], in_=grouped[i][:])

        def second_layer(i):
            first, blocks = units[i]
            e = first // 2
            sums[i] = psum.tile([P, 2, blocks * P], F32, name="sums%d" % i, tag=("bank2", "bank0", "bank1", "bank3", "bank4", "bank2", "bank0")[i])
            for a in range(2):
                nc.tensor.matmul_mx(
                    out=sums[i][:, a, :], lhsT=w2_w[e][:, 2 * a * P : 2 * (a + 1) * P].bitcast(FP4X4),
                    lhsT_scale=w2_s[:, e, a * P : (a + 1) * P],
                    rhs=codes[i][:].bitcast(FP8X4), rhs_scale=code_scales[i][:], start=True, stop=True,
                )

        out_rows = out.rearrange("(a n) j -> n a j", n=P)

        def store(i, copy):
            first, blocks = units[i]
            result = held.tile([P, 2, blocks * P], F32, name="result%d" % i)
            copy(result[:], sums[i][:])
            nc.sync.dma_start(out_rows[:, :, first * P : (first + blocks) * P], result[:])

        gather("token", "scales", 0, 4)
        gather("partner", "scales", 0, 4)
        gather("token", "words", 0, 2, lane_offset(1) - 256)
        gather("partner", "words", 0, 1, lane_offset(0) + 256)
        for j in range(BLOCKS):
            i = (j - 7) // 2
            finish = j >= 7 and j % 2 == 1
            if finish:
                quantise(i, j - 2)
            if j >= 1:
                gather_words(j)
                gather_scales(j)
            if j >= 2:
                turn((j - 2) // 2, j % 2)
            if j >= 3 and j % 2 == 1:
                group((j - 3) // 2, nc.vector.tensor_copy if j == BLOCKS - 1 else nc.scalar.copy)
            if finish:
                second_layer(i)
            first_layer(j)
            if finish:
                store(i, nc.vector.tensor_copy if j == BLOCKS - 1 else nc.scalar.copy)
        quantise(3, BLOCKS - 1, 0)
        turn(5, 0)
        second_layer(3)
        quantise(4, BLOCKS - 1)
        turn(6, 0)
        group(5, nc.scalar.copy)
        second_layer(4)
        quantise(5)
        group(6, nc.scalar.copy)
        quantise(6)
        store(3, nc.scalar.copy)
        store(4, nc.scalar.copy)
        second_layer(5)
        store(5, nc.vector.tensor_copy)
        second_layer(6)
        store(6, nc.vector.tensor_copy)
